import numpy as np
import ml_dtypes


def mxq(x, axis, fmt="e4m3"):
    dtype, down = {"e4m3": (ml_dtypes.float8_e4m3fn, 7), "e5m2": (ml_dtypes.float8_e5m2, 14)}[fmt]
    v = np.moveaxis(np.asarray(x, np.float32).astype(ml_dtypes.bfloat16).astype(np.float64), axis, -1)
    blocks = v.reshape(v.shape[:-1] + (-1, 32))
    amax = np.abs(blocks).max(-1, keepdims=True)
    byte = np.maximum(np.where(amax > 0, np.frexp(amax)[1] - 1 + 127, 0) - down, 1)
    scale = np.exp2(byte - 127.0)
    codes = (blocks / scale).astype(np.float32).astype(dtype).astype(np.float64)
    return np.moveaxis((codes * scale).reshape(v.shape), -1, axis)


WIDE = False


def mx_kscale(k):
    if not WIDE:
        return np.ones(k)
    levels = np.array([10, -10, 5, -5, 0])
    if k % 512:
        return np.exp2(np.random.permutation(np.resize(levels, k // 32))).repeat(32)
    a = np.empty((k // 512, 16))
    for p in range(k // 512):
        a[p, :8] = np.random.permutation(np.resize(levels, 8))
        for g in range(8):
            far = levels[np.abs(levels - a[p, g]) >= 10]
            a[p, g + 8] = far[np.random.randint(len(far))]
    return np.exp2(a.ravel()).repeat(32)


def f64(x):
    return np.asarray(x).astype(np.float64)


def striped(idx):
    return np.tile(idx.reshape(-1, 16).T, (8, 1)).astype(np.uint16)


def unstriped(offs):
    return offs[:16].T.reshape(-1).astype(np.int64)


E2M1 = np.array([0.0, 0.5, 1.0, 1.5, 2.0, 3.0, 4.0, 6.0, -0.0, -0.5, -1.0, -1.5, -2.0, -3.0, -4.0, -6.0])


def pack_weight(w, fmt):
    k, n = w.shape
    w = f64(np.asarray(w, np.float32).astype(ml_dtypes.bfloat16)).reshape(k // 32, 32, n)
    amax = np.abs(w).max(1)
    if fmt == "e4m3":
        byte = np.frexp(amax)[1] - 1 + 127 - 7
    else:
        mant, ex = np.frexp(amax / 6.0)
        byte = np.where(mant > 0.5, ex, ex - 1) + 127
    byte = np.clip(np.where(amax > 0, byte, 1), 1, 254)
    scaled = (w * np.exp2(127.0 - byte)[:, None, :]).reshape(k, n).astype(np.float32)
    by_word = np.ascontiguousarray(scaled.reshape(k // 512, 128, 4, n).transpose(0, 1, 3, 2))
    if fmt == "e4m3":
        words = by_word.astype(ml_dtypes.float8_e4m3fn).view(np.uint8)
    else:
        c = by_word.astype(ml_dtypes.float4_e2m1fn).view(np.uint8) & 0xF
        words = (c[..., 0::2] | (c[..., 1::2] << 4)).reshape(k // 512, 128, 2 * n)
    return np.ascontiguousarray(words), np.ascontiguousarray(byte.astype(np.uint8).reshape(k // 512, 16, n))


def unpack_weight(words, scales, fmt):
    g, _, n = scales.shape
    words = np.ascontiguousarray(words).reshape(g, 128, n, -1)
    if fmt == "e4m3":
        vals = words.view(ml_dtypes.float8_e4m3fn).astype(np.float64)
    else:
        nib = np.empty((g, 128, n, 4), np.uint8)
        nib[..., 0::2] = words & 0xF
        nib[..., 1::2] = words >> 4
        vals = E2M1[nib]
    vals = vals * np.repeat(np.exp2(scales.astype(np.float64) - 127.0), 8, axis=1)[..., None]
    return vals.transpose(0, 1, 3, 2).reshape(g * 512, n)


def silu(v):
    return v / (1.0 + np.exp(-np.maximum(v, -700.0)))


K, T, E, C, N = 2048, 2048, 2, 256, 512


def by_slot(wq, xq):
    return np.concatenate([xq[:, e * C:(e + 1) * C].T @ wq[e] for e in range(E)])


def setup_inputs():
    n = np.random.standard_normal
    s = mx_kscale(K)
    slot_token = np.concatenate([np.random.permutation(T)[:C] for e in range(E)])
    x = pack_weight(n((K, T)) * s[:, None], "e2m1")
    two = np.ascontiguousarray(x[0].reshape(K // 1024, 2, 128, T, 2).transpose(0, 2, 3, 1, 4).reshape(K // 1024, 128, T, 4))
    return {
        "x_words": two,
        "x_scales": x[1],
        "w": (n((E, K, N)) / np.sqrt(K) / s[None, :, None]).astype(np.float32),
        "w3": (n((E, K, N)) / np.sqrt(K) / s[None, :, None]).astype(np.float32),
        "offs": striped(slot_token),
    }


def reference(x_words, x_scales, w, w3, offs):
    wq = mxq(f64(w), 1, "e4m3")
    w3q = mxq(f64(w3), 1, "e4m3")
    idx = unstriped(offs)
    words = x_words.reshape(K // 1024, 128, T, 2, 2).transpose(0, 3, 1, 2, 4).reshape(K // 512, 128, 2 * T)
    xq = unpack_weight(words, x_scales, "e2m1")[:, idx]
    y = silu(by_slot(wq, xq)) * by_slot(w3q, xq)
    return y

@@ -1,0 +1,159 @@
+from contextlib import ExitStack
+
+import concourse.mybir as mybir
+
+K, T, E, C, N = 2048, 2048, 2, 256, 512
+FLOPS = 2 * 2 * E * C * K * N
+
+F32 = mybir.dt.float32
+BF16 = mybir.dt.bfloat16
+I32 = mybir.dt.int32
+U32 = mybir.dt.uint32
+U16 = mybir.dt.uint16
+U8 = mybir.dt.uint8
+FP8X4 = mybir.dt.float8_e4m3fn_x4
+FP4X4 = mybir.dt.float4_e2m1fn_x4
+
+P = 128
+PACK = 4
+K_PASS = P * PACK
+PASSES = K // K_PASS
+SLOTS = E * C
+BLOCKS = C // P
+NARROW = 128
+SCALAR_COLS = {512: 320, 256: 176, 128: 48}
+WIDE_LOADS = {("w", 0): (2, 2), ("w3", 0): (2, 2), ("w", 1): (2, 1, 1), ("w3", 1): (1,)}
+TAIL_PIECES = ((1, 0, 256), (2, 0, 256), (3, 0, 256), (1, 256, 512), (2, 256, 512), (3, 256, 384), (3, 384, 512))
+
+
+def interleave(copy, grouped, raw, c0, c1):
+    copy(
+        out=grouped[:, c0:c1, :].rearrange("p (c i) t -> p c t i", i=4),
+        in_=raw[:, :, c0:c1].rearrange("p t (c i) -> p c t i", i=4),
+    )
+
+
+def tile_moe_s_glu_silu_kernel(tc, x_words, x_scales, w, w3, offs, out):
+    nc = tc.nc
+    silu = mybir.ActivationFunctionType.Silu
+    mult = mybir.AluOpType.mult
+
+    with ExitStack() as ctx:
+        keep = ctx.enter_context(tc.tile_pool(name="keep", bufs=1))
+        stage = ctx.enter_context(tc.tile_pool(name="stage", bufs=4))
+        quant = ctx.enter_context(tc.tile_pool(name="quant", bufs=6))
+        psum = ctx.enter_context(tc.psum_pool(name="psum", bufs=8))
+
+        offsets = keep.tile([P, SLOTS // 16], U16, name="offsets")
+        word_window = keep.tile([P, 2, T], I32, name="word_window")
+        scale_window = keep.tile([P, PASSES, T // 4], I32, name="scale_window")
+        nc.vector.memset(scale_window[:], 0)
+
+        nc.sync.dma_start(word_window[:], x_words.rearrange("m p t d -> p m (t d)").bitcast(I32))
+        nc.sync.dma_start(offsets[:], offs)
+        scale_rows = x_scales.bitcast(I32).rearrange("s (q r) t -> r q s t", r=4)
+        for r in range(4):
+            nc.gpsimd.dma_start(scale_window[r:P:32, :, :], scale_rows[r])
+
+        raws = {}
+        for e in range(E):
+            for name, mat in (("w", w), ("w3", w3)):
+                rows = mat[e].rearrange("(g p j) n -> p g j n", p=P, j=PACK)
+                g0 = 0
+                for count in WIDE_LOADS[name, e]:
+                    raw = keep.tile([P, count, PACK, N], F32, name=f"raw_{name}_{e}_{g0}")
+                    nc.sync.dma_start(raw[:], rows[:, g0 : g0 + count, :, :])
+                    for i in range(count):
+                        raws[name, e, g0 + i, 0] = raw[:, i, :, :]
+                    g0 += count
+        rows = w3[E - 1].rearrange("(g p j) n -> p g j n", p=P, j=PACK)
+        for g, c0, c1 in TAIL_PIECES:
+            raw = keep.tile([P, PACK, c1 - c0], F32, name=f"raw_tail_{g}_{c0}")
+            nc.sync.dma_start(raw[:], rows[:, g, :, c0:c1])
+            raws["w3", E - 1, g, c0] = raw[:]
+
+        tok_words = keep.tile([P, PASSES, 2 * SLOTS], U8, name="tok_words", align_bytes=64)
+        tok_scales = keep.tile([P, PASSES, SLOTS], U8, name="tok_scales", align_bytes=64)
+        scale_bytes = scale_window[:].rearrange("p s t -> p (s t)").bitcast(U8)
+        for m in range(2):
+            pair = keep.tile([P, SLOTS], U32, name=f"pair{m}")
+            nc.vector.tensor_copy(pair[:], word_window[:, m, :].bitcast(U32).indirect(offsets[:]))
+            for s in (2 * m, 2 * m + 1):
+                nc.vector.tensor_copy(tok_scales[:, s, :], scale_bytes[:, s * T : (s + 1) * T].indirect(offsets[:]))
+            nc.vector.tensor_copy(
+                tok_words[:, 2 * m : 2 * m + 2, :].bitcast(U16),
+                pair[:].bitcast(U16).rearrange("p (n q) -> p q n", q=2),
+            )
+
+        def quantize(raw, width):
+            grouped = stage.tile([P, width, PACK], BF16, name="grouped", align_bytes=64)
+            split = SCALAR_COLS[width]
+            interleave(nc.scalar.copy, grouped, raw, 0, split)
+            interleave(nc.vector.tensor_copy, grouped, raw, split, width)
+            codes = quant.tile([P, width], U32, name="codes", align_bytes=64)
+            scales = quant.tile([P, width], U8, name="scales", align_bytes=64)
+            nc.vector.quantize_mx(
+                out=codes[:].bitcast(FP8X4), scales=scales[:], in_=grouped[:].rearrange("p n t -> p (n t)")
+            )
+            return codes, scales
+
+        def multiply(acc, e, b, g, codes, scales):
+            s0 = e * C + b * P
+            nc.tensor.matmul_mx(
+                out=acc,
+                lhsT=tok_words[:, g, 2 * s0 : 2 * (s0 + P)].bitcast(FP4X4),
+                lhsT_scale=tok_scales[:, g, s0 : s0 + P],
+                rhs=codes.bitcast(FP8X4),
+                rhs_scale=scales,
+                start=(g == 0),
+                stop=(g == PASSES - 1),
+            )
+
+        def wide_product(name, e):
+            accs = [psum.tile([P, N], F32, name="acc") for b in range(BLOCKS)]
+            for g in range(PASSES):
+                codes, scales = quantize(raws[name, e, g, 0], N)
+                for b in range(BLOCKS):
+                    multiply(accs[b][:], e, b, g, codes[:], scales[:])
+            return accs
+
+        def gate(e):
+            accs = wide_product("w", e)
+            gated = keep.tile([P, BLOCKS, N], F32, name=f"gated{e}")
+            for b in range(BLOCKS):
+                nc.scalar.activation(gated[:, b, :], accs[b][:], silu)
+            return gated
+
+        def store(e, result, c0, c1):
+            nc.sync.dma_start(out[e * C : (e + 1) * C, c0:c1].rearrange("(b p) n -> p b n", p=P), result[:])
+
+        for e in range(E - 1):
+            gated = gate(e)
+            accs = wide_product("w3", e)
+            result = keep.tile([P, BLOCKS, N], F32, name=f"result{e}")
+            for b in range(BLOCKS):
+                nc.vector.tensor_tensor(result[:, b, :], accs[b][:], gated[:, b, :], mult)
+            store(e, result, 0, N)
+
+        e = E - 1
+        gated = gate(e)
+        chunks = range(N // NARROW)
+        accs = {(c, b): psum.tile([P, NARROW], F32, name="acc") for c in chunks for b in range(BLOCKS)}
+        for g, c0, c1 in ((0, 0, N),) + TAIL_PIECES:
+            codes, scales = quantize(raws["w3", e, g, c0], c1 - c0)
+            starts = range(c0, c1, NARROW)
+            for n0 in starts:
+                cols = slice(n0 - c0, n0 - c0 + NARROW)
+                for b in range(BLOCKS):
+                    multiply(accs[n0 // NARROW, b][:], e, b, g, codes[:, cols], scales[:, cols])
+            if g == PASSES - 1:
+                result = keep.tile([P, BLOCKS, c1 - c0], F32, name=f"result_tail{c0}")
+                for n0 in starts:
+                    for b in range(BLOCKS):
+                        nc.vector.tensor_tensor(
+                            result[:, b, n0 - c0 : n0 - c0 + NARROW],
+                            accs[n0 // NARROW, b][:],
+                            gated[:, b, n0 : n0 + NARROW],
+                            mult,
+                        )
+                store(e, result, c0, c1)

@@ -53,7 +53,7 @@ def tile_moe_s_glu_silu_kernel(tc, x_words, x_scales, w, w3, offs, out):
         nc.sync.dma_start(offsets[:], offs)
         scale_rows = x_scales.bitcast(I32).rearrange("s (q r) t -> r q s t", r=4)
         for r in range(4):
-            nc.gpsimd.dma_start(scale_window[r:P:32, :, :], scale_rows[r])
+            nc.sync.dma_start(scale_window[r:P:32, :, :], scale_rows[r])
 
         raws = {}
         for e in range(E):

@@ -22,7 +22,6 @@ SLOTS = E * C
 BLOCKS = C // P
 NARROW = 128
 SCALAR_COLS = {512: 320, 256: 176, 128: 48}
-WIDE_LOADS = {("w", 0): (2, 2), ("w3", 0): (2, 2), ("w", 1): (2, 1, 1), ("w3", 1): (1,)}
 TAIL_PIECES = ((1, 0, 256), (2, 0, 256), (3, 0, 256), (1, 256, 512), (2, 256, 512), (3, 256, 384), (3, 384, 512))
 
 
@@ -41,7 +40,8 @@ def tile_moe_s_glu_silu_kernel(tc, x_words, x_scales, w, w3, offs, out):
     with ExitStack() as ctx:
         keep = ctx.enter_context(tc.tile_pool(name="keep", bufs=1))
         stage = ctx.enter_context(tc.tile_pool(name="stage", bufs=4))
-        quant = ctx.enter_context(tc.tile_pool(name="quant", bufs=6))
+        quant = ctx.enter_context(tc.tile_pool(name="quant", bufs=14))
+        stream = ctx.enter_context(tc.tile_pool(name="stream", bufs=5))
         psum = ctx.enter_context(tc.psum_pool(name="psum", bufs=8))
 
         offsets = keep.tile([P, SLOTS // 16], U16, name="offsets")
@@ -49,41 +49,46 @@ def tile_moe_s_glu_silu_kernel(tc, x_words, x_scales, w, w3, offs, out):
         scale_window = keep.tile([P, PASSES, T // 4], I32, name="scale_window")
         nc.vector.memset(scale_window[:], 0)
 
-        nc.sync.dma_start(word_window[:], x_words.rearrange("m p t d -> p m (t d)").bitcast(I32))
+        tok_scales = keep.tile([P, PASSES, SLOTS // 4], I32, name="tok_scales", align_bytes=64)
+        nc.vector.memset(tok_scales[:], 0)
+
+        nc.scalar.dma_start(scale_window[4:P:8, :, :], x_scales.bitcast(I32).rearrange("s b t -> b s t"))
         nc.sync.dma_start(offsets[:], offs)
-        scale_rows = x_scales.bitcast(I32).rearrange("s (q r) t -> r q s t", r=4)
-        for r in range(4):
-            nc.sync.dma_start(scale_window[r:P:32, :, :], scale_rows[r])
 
         raws = {}
+
+        def load(name, mat, e, g, c0, c1):
+            rows = mat[e].rearrange("(g p j) n -> p g j n", p=P, j=PACK)
+            raw = stream.tile([P, PACK, c1 - c0], F32, name="raw")
+            nc.sync.dma_start(raw[:], rows[:, g, :, c0:c1])
+            raws[name, e, g, c0] = raw[:]
+
         for e in range(E):
             for name, mat in (("w", w), ("w3", w3)):
-                rows = mat[e].rearrange("(g p j) n -> p g j n", p=P, j=PACK)
-                g0 = 0
-                for count in WIDE_LOADS[name, e]:
-                    raw = keep.tile([P, count, PACK, N], F32, name=f"raw_{name}_{e}_{g0}")
-                    nc.sync.dma_start(raw[:], rows[:, g0 : g0 + count, :, :])
-                    for i in range(count):
-                        raws[name, e, g0 + i, 0] = raw[:, i, :, :]
-                    g0 += count
-        rows = w3[E - 1].rearrange("(g p j) n -> p g j n", p=P, j=PACK)
-        for g, c0, c1 in TAIL_PIECES:
-            raw = keep.tile([P, PACK, c1 - c0], F32, name=f"raw_tail_{g}_{c0}")
-            nc.sync.dma_start(raw[:], rows[:, g, :, c0:c1])
-            raws["w3", E - 1, g, c0] = raw[:]
+                if (name, e) == ("w3", E - 1):
+                    for g, c0, c1 in ((0, 0, N),) + TAIL_PIECES:
+                        load(name, mat, e, g, c0, c1)
+                else:
+                    for g in range(PASSES):
+                        load(name, mat, e, g, 0, N)
+                        if (name, e, g) == ("w", 0, 0):
+                            nc.sync.dma_start(word_window[:], x_words.rearrange("m p t d -> p m (t d)").bitcast(I32))
 
         tok_words = keep.tile([P, PASSES, 2 * SLOTS], U8, name="tok_words", align_bytes=64)
-        tok_scales = keep.tile([P, PASSES, SLOTS], U8, name="tok_scales", align_bytes=64)
+        picked_scales = keep.tile([P, PASSES, SLOTS], U8, name="picked_scales")
         scale_bytes = scale_window[:].rearrange("p s t -> p (s t)").bitcast(U8)
+        for s in range(PASSES):
+            nc.vector.tensor_copy(picked_scales[:, s, :], scale_bytes[:, s * T : (s + 1) * T].indirect(offsets[:]))
+        for r in range(4):
+            nc.scalar.dma_start(tok_scales[r:P:32, :, :], picked_scales[4 + 8 * r : P : 32, :, :].bitcast(I32))
         for m in range(2):
             pair = keep.tile([P, SLOTS], U32, name=f"pair{m}")
             nc.vector.tensor_copy(pair[:], word_window[:, m, :].bitcast(U32).indirect(offsets[:]))
-            for s in (2 * m, 2 * m + 1):
-                nc.vector.tensor_copy(tok_scales[:, s, :], scale_bytes[:, s * T : (s + 1) * T].indirect(offsets[:]))
             nc.vector.tensor_copy(
                 tok_words[:, 2 * m : 2 * m + 2, :].bitcast(U16),
                 pair[:].bitcast(U16).rearrange("p (n q) -> p q n", q=2),
             )
+        tok_scale_bytes = tok_scales[:].bitcast(U8)
 
         def quantize(raw, width):
             grouped = stage.tile([P, width, PACK], BF16, name="grouped", align_bytes=64)
@@ -102,7 +107,7 @@ def tile_moe_s_glu_silu_kernel(tc, x_words, x_scales, w, w3, offs, out):
             nc.tensor.matmul_mx(
                 out=acc,
                 lhsT=tok_words[:, g, 2 * s0 : 2 * (s0 + P)].bitcast(FP4X4),
-                lhsT_scale=tok_scales[:, g, s0 : s0 + P],
+                lhsT_scale=tok_scale_bytes[:, g, s0 : s0 + P],
                 rhs=codes.bitcast(FP8X4),
                 rhs_scale=scales,
                 start=(g == 0),
@@ -124,16 +129,14 @@ def tile_moe_s_glu_silu_kernel(tc, x_words, x_scales, w, w3, offs, out):
                 nc.scalar.activation(gated[:, b, :], accs[b][:], silu)
             return gated
 
-        def store(e, result, c0, c1):
-            nc.sync.dma_start(out[e * C : (e + 1) * C, c0:c1].rearrange("(b p) n -> p b n", p=P), result[:])
+        result = keep.tile([P, E * BLOCKS, N], F32, name="result")
+        out_rows = out.rearrange("(b p) n -> p b n", p=P)
 
         for e in range(E - 1):
             gated = gate(e)
             accs = wide_product("w3", e)
-            result = keep.tile([P, BLOCKS, N], F32, name=f"result{e}")
             for b in range(BLOCKS):
-                nc.vector.tensor_tensor(result[:, b, :], accs[b][:], gated[:, b, :], mult)
-            store(e, result, 0, N)
+                nc.vector.tensor_tensor(result[:, e * BLOCKS + b, :], accs[b][:], gated[:, b, :], mult)
 
         e = E - 1
         gated = gate(e)
@@ -147,13 +150,12 @@ def tile_moe_s_glu_silu_kernel(tc, x_words, x_scales, w, w3, offs, out):
                 for b in range(BLOCKS):
                     multiply(accs[n0 // NARROW, b][:], e, b, g, codes[:, cols], scales[:, cols])
             if g == PASSES - 1:
-                result = keep.tile([P, BLOCKS, c1 - c0], F32, name=f"result_tail{c0}")
                 for n0 in starts:
                     for b in range(BLOCKS):
                         nc.vector.tensor_tensor(
-                            result[:, b, n0 - c0 : n0 - c0 + NARROW],
+                            result[:, e * BLOCKS + b, n0 : n0 + NARROW],
                             accs[n0 // NARROW, b][:],
                             gated[:, b, n0 : n0 + NARROW],
                             mult,
                         )
-                store(e, result, c0, c1)
+                nc.sync.dma_start(out_rows[:, :, c0:c1], result[:, :, c0:c1])

@@ -21,8 +21,10 @@ PASSES = K // K_PASS
 SLOTS = E * C
 BLOCKS = C // P
 NARROW = 128
-SCALAR_COLS = {512: 320, 256: 176, 128: 48}
-TAIL_PIECES = ((1, 0, 256), (2, 0, 256), (3, 0, 256), (1, 256, 512), (2, 256, 512), (3, 256, 384), (3, 384, 512))
+WIDE_SCALAR_COLS = 304
+W_LOADS = (1, 2, 2, 2, 1)
+W3_LOADS = (2, 2, 1, 1, 1)
+HALF = N // 2
 
 
 def interleave(copy, grouped, raw, c0, c1):
@@ -40,7 +42,7 @@ def tile_moe_s_glu_silu_kernel(tc, x_words, x_scales, w, w3, offs, out):
     with ExitStack() as ctx:
         keep = ctx.enter_context(tc.tile_pool(name="keep", bufs=1))
         stage = ctx.enter_context(tc.tile_pool(name="stage", bufs=4))
-        quant = ctx.enter_context(tc.tile_pool(name="quant", bufs=14))
+        quant = ctx.enter_context(tc.tile_pool(name="quant", bufs=10))
         stream = ctx.enter_context(tc.tile_pool(name="stream", bufs=5))
         psum = ctx.enter_context(tc.psum_pool(name="psum", bufs=8))
 
@@ -53,26 +55,30 @@ def tile_moe_s_glu_silu_kernel(tc, x_words, x_scales, w, w3, offs, out):
         nc.vector.memset(tok_scales[:], 0)
 
         nc.scalar.dma_start(scale_window[4:P:8, :, :], x_scales.bitcast(I32).rearrange("s b t -> b s t"))
-        nc.sync.dma_start(offsets[:], offs)
 
         raws = {}
 
-        def load(name, mat, e, g, c0, c1):
-            rows = mat[e].rearrange("(g p j) n -> p g j n", p=P, j=PACK)
-            raw = stream.tile([P, PACK, c1 - c0], F32, name="raw")
-            nc.sync.dma_start(raw[:], rows[:, g, :, c0:c1])
-            raws[name, e, g, c0] = raw[:]
+        def load_wide(name, mat, first, count):
+            rows = mat.rearrange("e (g p j) n -> p (e g) j n", p=P, j=PACK)
+            raw = stream.tile([P, count, PACK, N], F32, name="raw")
+            nc.sync.dma_start(raw[:], rows[:, first : first + count, :, :])
+            for i in range(count):
+                e, g = divmod(first + i, PASSES)
+                raws[name, e, g, 0] = raw[:, i, :, :]
 
-        for e in range(E):
-            for name, mat in (("w", w), ("w3", w3)):
-                if (name, e) == ("w3", E - 1):
-                    for g, c0, c1 in ((0, 0, N),) + TAIL_PIECES:
-                        load(name, mat, e, g, c0, c1)
-                else:
-                    for g in range(PASSES):
-                        load(name, mat, e, g, 0, N)
-                        if (name, e, g) == ("w", 0, 0):
-                            nc.sync.dma_start(word_window[:], x_words.rearrange("m p t d -> p m (t d)").bitcast(I32))
+        for name, mat, counts in (("w", w, W_LOADS), ("w3", w3, W3_LOADS)):
+            first = 0
+            for count in counts:
+                load_wide(name, mat, first, count)
+                if (name, first) == ("w", 0):
+                    nc.sync.dma_start(offsets[:], offs)
+                    nc.sync.dma_start(word_window[:], x_words.rearrange("m p t d -> p m (t d)").bitcast(I32))
+                first += count
+        last_rows = w3[E - 1, K - K_PASS :, :].rearrange("(p j) n -> p j n", j=PACK)
+        halves = {}
+        for h0 in (0, HALF):
+            halves[h0] = stream.tile([P, PACK, HALF], F32, name="raw")
+            nc.sync.dma_start(halves[h0][:], last_rows[:, :, h0 : h0 + HALF])
 
         tok_words = keep.tile([P, PASSES, 2 * SLOTS], U8, name="tok_words", align_bytes=64)
         picked_scales = keep.tile([P, PASSES, SLOTS], U8, name="picked_scales")
@@ -90,11 +96,12 @@ def tile_moe_s_glu_silu_kernel(tc, x_words, x_scales, w, w3, offs, out):
             )
         tok_scale_bytes = tok_scales[:].bitcast(U8)
 
-        def quantize(raw, width):
+        def quantize(raw, width, split):
             grouped = stage.tile([P, width, PACK], BF16, name="grouped", align_bytes=64)
-            split = SCALAR_COLS[width]
-            interleave(nc.scalar.copy, grouped, raw, 0, split)
-            interleave(nc.vector.tensor_copy, grouped, raw, split, width)
+            if split > 0:
+                interleave(nc.scalar.copy, grouped, raw, 0, split)
+            if split < width:
+                interleave(nc.vector.tensor_copy, grouped, raw, split, width)
             codes = quant.tile([P, width], U32, name="codes", align_bytes=64)
             scales = quant.tile([P, width], U8, name="scales", align_bytes=64)
             nc.vector.quantize_mx(
@@ -117,7 +124,7 @@ def tile_moe_s_glu_silu_kernel(tc, x_words, x_scales, w, w3, offs, out):
         def wide_product(name, e):
             accs = [psum.tile([P, N], F32, name="acc") for b in range(BLOCKS)]
             for g in range(PASSES):
-                codes, scales = quantize(raws[name, e, g, 0], N)
+                codes, scales = quantize(raws[name, e, g, 0], N, WIDE_SCALAR_COLS)
                 for b in range(BLOCKS):
                     multiply(accs[b][:], e, b, g, codes[:], scales[:])
             return accs
@@ -132,30 +139,40 @@ def tile_moe_s_glu_silu_kernel(tc, x_words, x_scales, w, w3, offs, out):
         result = keep.tile([P, E * BLOCKS, N], F32, name="result")
         out_rows = out.rearrange("(b p) n -> p b n", p=P)
 
+        gates = [gate(e) for e in range(E)]
         for e in range(E - 1):
-            gated = gate(e)
             accs = wide_product("w3", e)
             for b in range(BLOCKS):
-                nc.vector.tensor_tensor(result[:, e * BLOCKS + b, :], accs[b][:], gated[:, b, :], mult)
+                nc.vector.tensor_tensor(result[:, e * BLOCKS + b, :], accs[b][:], gates[e][:, b, :], mult)
+            nc.sync.dma_start(out_rows[:, e * BLOCKS : (e + 1) * BLOCKS, :], result[:, e * BLOCKS : (e + 1) * BLOCKS, :])
 
         e = E - 1
-        gated = gate(e)
+        gated = gates[e]
         chunks = range(N // NARROW)
         accs = {(c, b): psum.tile([P, NARROW], F32, name="acc") for c in chunks for b in range(BLOCKS)}
-        for g, c0, c1 in ((0, 0, N),) + TAIL_PIECES:
-            codes, scales = quantize(raws["w3", e, g, c0], c1 - c0)
-            starts = range(c0, c1, NARROW)
-            for n0 in starts:
-                cols = slice(n0 - c0, n0 - c0 + NARROW)
+
+        def multiply_narrow(g, n0, codes, scales):
+            for b in range(BLOCKS):
+                multiply(accs[n0 // NARROW, b][:], e, b, g, codes, scales)
+
+        for g in range(PASSES - 1):
+            codes, scales = quantize(raws["w3", e, g, 0], N, WIDE_SCALAR_COLS)
+            for n0 in range(0, N, NARROW):
+                multiply_narrow(g, n0, codes[:, n0 : n0 + NARROW], scales[:, n0 : n0 + NARROW])
+        rows = slice(e * BLOCKS, (e + 1) * BLOCKS)
+        for h0 in (0, HALF):
+            for c0, split in ((0, 0), (NARROW, NARROW)):
+                codes, scales = quantize(halves[h0][:, :, c0 : c0 + NARROW], NARROW, split)
+                multiply_narrow(PASSES - 1, h0 + c0, codes[:], scales[:])
+            for n0 in (h0, h0 + NARROW):
                 for b in range(BLOCKS):
-                    multiply(accs[n0 // NARROW, b][:], e, b, g, codes[:, cols], scales[:, cols])
-            if g == PASSES - 1:
-                for n0 in starts:
-                    for b in range(BLOCKS):
-                        nc.vector.tensor_tensor(
-                            result[:, e * BLOCKS + b, n0 : n0 + NARROW],
-                            accs[n0 // NARROW, b][:],
-                            gated[:, b, n0 : n0 + NARROW],
-                            mult,
-                        )
-                nc.sync.dma_start(out_rows[:, :, c0:c1], result[:, :, c0:c1])
+                    nc.vector.tensor_tensor(
+                        result[:, e * BLOCKS + b, n0 : n0 + NARROW],
+                        accs[n0 // NARROW, b][:],
+                        gated[:, b, n0 : n0 + NARROW],
+                        mult,
+                    )
+                if h0 == HALF:
+                    nc.sync.dma_start(out_rows[:, rows, n0 : n0 + NARROW], result[:, rows, n0 : n0 + NARROW])
+            if h0 == 0:
+                nc.sync.dma_start(out_rows[:, rows, 0:HALF], result[:, rows, 0:HALF])

from contextlib import ExitStack

import concourse.mybir as mybir

K, T, E, C, N = 2048, 2048, 2, 256, 512
FLOPS = 2 * 2 * E * C * K * N

F32 = mybir.dt.float32
BF16 = mybir.dt.bfloat16
I32 = mybir.dt.int32
U32 = mybir.dt.uint32
U16 = mybir.dt.uint16
U8 = mybir.dt.uint8
FP8X4 = mybir.dt.float8_e4m3fn_x4
FP4X4 = mybir.dt.float4_e2m1fn_x4

P = 128
PACK = 4
K_PASS = P * PACK
PASSES = K // K_PASS
SLOTS = E * C
BLOCKS = C // P
NARROW = 128
WIDE_SCALAR_COLS = 304
W_LOADS = (1, 2, 2, 2, 1)
W3_LOADS = (2, 2, 1, 1, 1)
HALF = N // 2


def interleave(copy, grouped, raw, c0, c1):
    copy(
        out=grouped[:, c0:c1, :].rearrange("p (c i) t -> p c t i", i=4),
        in_=raw[:, :, c0:c1].rearrange("p t (c i) -> p c t i", i=4),
    )


def tile_moe_s_glu_silu_kernel(tc, x_words, x_scales, w, w3, offs, out):
    nc = tc.nc
    silu = mybir.ActivationFunctionType.Silu
    mult = mybir.AluOpType.mult

    with ExitStack() as ctx:
        keep = ctx.enter_context(tc.tile_pool(name="keep", bufs=1))
        stage = ctx.enter_context(tc.tile_pool(name="stage", bufs=4))
        quant = ctx.enter_context(tc.tile_pool(name="quant", bufs=10))
        stream = ctx.enter_context(tc.tile_pool(name="stream", bufs=5))
        psum = ctx.enter_context(tc.psum_pool(name="psum", bufs=8))

        offsets = keep.tile([P, SLOTS // 16], U16, name="offsets")
        word_window = keep.tile([P, 2, T], I32, name="word_window")
        scale_window = keep.tile([P, PASSES, T // 4], I32, name="scale_window")
        nc.vector.memset(scale_window[:], 0)

        tok_scales = keep.tile([P, PASSES, SLOTS // 4], I32, name="tok_scales", align_bytes=64)
        nc.vector.memset(tok_scales[:], 0)

        nc.scalar.dma_start(scale_window[4:P:8, :, :], x_scales.bitcast(I32).rearrange("s b t -> b s t"))

        raws = {}

        def load_wide(name, mat, first, count):
            rows = mat.rearrange("e (g p j) n -> p (e g) j n", p=P, j=PACK)
            raw = stream.tile([P, count, PACK, N], F32, name="raw")
            nc.sync.dma_start(raw[:], rows[:, first : first + count, :, :])
            for i in range(count):
                e, g = divmod(first + i, PASSES)
                raws[name, e, g, 0] = raw[:, i, :, :]

        for name, mat, counts in (("w", w, W_LOADS), ("w3", w3, W3_LOADS)):
            first = 0
            for count in counts:
                load_wide(name, mat, first, count)
                if (name, first) == ("w", 0):
                    nc.sync.dma_start(offsets[:], offs)
                    nc.sync.dma_start(word_window[:], x_words.rearrange("m p t d -> p m (t d)").bitcast(I32))
                first += count
        last_rows = w3[E - 1, K - K_PASS :, :].rearrange("(p j) n -> p j n", j=PACK)
        halves = {}
        for h0 in (0, HALF):
            halves[h0] = stream.tile([P, PACK, HALF], F32, name="raw")
            nc.sync.dma_start(halves[h0][:], last_rows[:, :, h0 : h0 + HALF])

        tok_words = keep.tile([P, PASSES, 2 * SLOTS], U8, name="tok_words", align_bytes=64)
        picked_scales = keep.tile([P, PASSES, SLOTS], U8, name="picked_scales")
        scale_bytes = scale_window[:].rearrange("p s t -> p (s t)").bitcast(U8)
        for s in range(PASSES):
            nc.vector.tensor_copy(picked_scales[:, s, :], scale_bytes[:, s * T : (s + 1) * T].indirect(offsets[:]))
        for r in range(4):
            nc.scalar.dma_start(tok_scales[r:P:32, :, :], picked_scales[4 + 8 * r : P : 32, :, :].bitcast(I32))
        for m in range(2):
            pair = keep.tile([P, SLOTS], U32, name=f"pair{m}")
            nc.vector.tensor_copy(pair[:], word_window[:, m, :].bitcast(U32).indirect(offsets[:]))
            nc.vector.tensor_copy(
                tok_words[:, 2 * m : 2 * m + 2, :].bitcast(U16),
                pair[:].bitcast(U16).rearrange("p (n q) -> p q n", q=2),
            )
        tok_scale_bytes = tok_scales[:].bitcast(U8)

        def quantize(raw, width, split):
            grouped = stage.tile([P, width, PACK], BF16, name="grouped", align_bytes=64)
            if split > 0:
                interleave(nc.scalar.copy, grouped, raw, 0, split)
            if split < width:
                interleave(nc.vector.tensor_copy, grouped, raw, split, width)
            codes = quant.tile([P, width], U32, name="codes", align_bytes=64)
            scales = quant.tile([P, width], U8, name="scales", align_bytes=64)
            nc.vector.quantize_mx(
                out=codes[:].bitcast(FP8X4), scales=scales[:], in_=grouped[:].rearrange("p n t -> p (n t)")
            )
            return codes, scales

        def multiply(acc, e, b, g, codes, scales):
            s0 = e * C + b * P
            nc.tensor.matmul_mx(
                out=acc,
                lhsT=tok_words[:, g, 2 * s0 : 2 * (s0 + P)].bitcast(FP4X4),
                lhsT_scale=tok_scale_bytes[:, g, s0 : s0 + P],
                rhs=codes.bitcast(FP8X4),
                rhs_scale=scales,
                start=(g == 0),
                stop=(g == PASSES - 1),
            )

        def wide_product(name, e):
            accs = [psum.tile([P, N], F32, name="acc") for b in range(BLOCKS)]
            for g in range(PASSES):
                codes, scales = quantize(raws[name, e, g, 0], N, WIDE_SCALAR_COLS)
                for b in range(BLOCKS):
                    multiply(accs[b][:], e, b, g, codes[:], scales[:])
            return accs

        def gate(e):
            accs = wide_product("w", e)
            gated = keep.tile([P, BLOCKS, N], F32, name=f"gated{e}")
            for b in range(BLOCKS):
                nc.scalar.activation(gated[:, b, :], accs[b][:], silu)
            return gated

        result = keep.tile([P, E * BLOCKS, N], F32, name="result")
        out_rows = out.rearrange("(b p) n -> p b n", p=P)

        gates = [gate(e) for e in range(E)]
        for e in range(E - 1):
            accs = wide_product("w3", e)
            for b in range(BLOCKS):
                nc.vector.tensor_tensor(result[:, e * BLOCKS + b, :], accs[b][:], gates[e][:, b, :], mult)
            nc.sync.dma_start(out_rows[:, e * BLOCKS : (e + 1) * BLOCKS, :], result[:, e * BLOCKS : (e + 1) * BLOCKS, :])

        e = E - 1
        gated = gates[e]
        chunks = range(N // NARROW)
        accs = {(c, b): psum.tile([P, NARROW], F32, name="acc") for c in chunks for b in range(BLOCKS)}

        def multiply_narrow(g, n0, codes, scales):
            for b in range(BLOCKS):
                multiply(accs[n0 // NARROW, b][:], e, b, g, codes, scales)

        for g in range(PASSES - 1):
            codes, scales = quantize(raws["w3", e, g, 0], N, WIDE_SCALAR_COLS)
            for n0 in range(0, N, NARROW):
                multiply_narrow(g, n0, codes[:, n0 : n0 + NARROW], scales[:, n0 : n0 + NARROW])
        rows = slice(e * BLOCKS, (e + 1) * BLOCKS)
        for h0 in (0, HALF):
            for c0, split in ((0, 0), (NARROW, NARROW)):
                codes, scales = quantize(halves[h0][:, :, c0 : c0 + NARROW], NARROW, split)
                multiply_narrow(PASSES - 1, h0 + c0, codes[:], scales[:])
            for n0 in (h0, h0 + NARROW):
                for b in range(BLOCKS):
                    nc.vector.tensor_tensor(
                        result[:, e * BLOCKS + b, n0 : n0 + NARROW],
                        accs[n0 // NARROW, b][:],
                        gated[:, b, n0 : n0 + NARROW],
                        mult,
                    )
                if h0 == HALF:
                    nc.sync.dma_start(out_rows[:, rows, n0 : n0 + NARROW], result[:, rows, n0 : n0 + NARROW])
            if h0 == 0:
                nc.sync.dma_start(out_rows[:, rows, 0:HALF], result[:, rows, 0:HALF])
